import numpy as np
import ml_dtypes


def mxq(x, axis, fmt="e4m3"):
    dtype, down = {"e4m3": (ml_dtypes.float8_e4m3fn, 7), "e5m2": (ml_dtypes.float8_e5m2, 14)}[fmt]
    v = np.moveaxis(np.asarray(x, np.float32).astype(ml_dtypes.bfloat16).astype(np.float64), axis, -1)
    blocks = v.reshape(v.shape[:-1] + (-1, 32))
    amax = np.abs(blocks).max(-1, keepdims=True)
    byte = np.maximum(np.where(amax > 0, np.frexp(amax)[1] - 1 + 127, 0) - down, 1)
    scale = np.exp2(byte - 127.0)
    codes = (blocks / scale).astype(np.float32).astype(dtype).astype(np.float64)
    return np.moveaxis((codes * scale).reshape(v.shape), -1, axis)


WIDE = False


def mx_kscale(k):
    if not WIDE:
        return np.ones(k)
    levels = np.array([30, -30])
    if k % 512:
        return np.exp2(np.random.permutation(np.resize(levels, k // 32))).repeat(32)
    a = np.empty((k // 512, 16))
    for p in range(k // 512):
        a[p, :8] = np.random.permutation(np.resize(levels, 8))
        for g in range(8):
            far = levels[np.abs(levels - a[p, g]) >= 10]
            a[p, g + 8] = far[np.random.randint(len(far))]
    return np.exp2(a.ravel()).repeat(32)


def f64(x):
    return np.asarray(x).astype(np.float64)


def striped(idx):
    return np.tile(np.asarray(idx).reshape(-1, 16).T, (8, 1)).astype(np.uint16)


def unstriped(offs):
    return offs[:16].T.reshape(-1).astype(np.int64)


E2M1 = np.array([0.0, 0.5, 1.0, 1.5, 2.0, 3.0, 4.0, 6.0, -0.0, -0.5, -1.0, -1.5, -2.0, -3.0, -4.0, -6.0])


def pack_weight(w, fmt):
    k, n = w.shape
    w = f64(np.asarray(w, np.float32).astype(ml_dtypes.bfloat16)).reshape(k // 32, 32, n)
    amax = np.abs(w).max(1)
    if fmt in ("e4m3", "e5m2"):
        byte = np.frexp(amax)[1] - 1 + 127 - (7 if fmt == "e4m3" else 14)
    else:
        mant, ex = np.frexp(amax / 6.0)
        byte = np.where(mant > 0.5, ex, ex - 1) + 127
    byte = np.clip(np.where(amax > 0, byte, 1), 1, 254)
    scaled = (w * np.exp2(127.0 - byte)[:, None, :]).reshape(k, n).astype(np.float32)
    by_word = np.ascontiguousarray(scaled.reshape(k // 512, 128, 4, n).transpose(0, 1, 3, 2))
    if fmt in ("e4m3", "e5m2"):
        words = by_word.astype(ml_dtypes.float8_e4m3fn if fmt == "e4m3" else ml_dtypes.float8_e5m2).view(np.uint8)
    else:
        c = by_word.astype(ml_dtypes.float4_e2m1fn).view(np.uint8) & 0xF
        words = (c[..., 0::2] | (c[..., 1::2] << 4)).reshape(k // 512, 128, 2 * n)
    return np.ascontiguousarray(words), np.ascontiguousarray(byte.astype(np.uint8).reshape(k // 512, 16, n))


def unpack_weight(words, scales, fmt):
    g, _, n = scales.shape
    words = np.ascontiguousarray(words).reshape(g, 128, n, -1)
    if fmt in ("e4m3", "e5m2"):
        vals = words.view(ml_dtypes.float8_e4m3fn if fmt == "e4m3" else ml_dtypes.float8_e5m2).astype(np.float64)
    else:
        nib = np.empty((g, 128, n, 4), np.uint8)
        nib[..., 0::2] = words & 0xF
        nib[..., 1::2] = words >> 4
        vals = E2M1[nib]
    vals = vals * np.repeat(np.exp2(scales.astype(np.float64) - 127.0), 8, axis=1)[..., None]
    return vals.transpose(0, 1, 3, 2).reshape(g * 512, n)


def sigmoid(v):
    return 1.0 / (1.0 + np.exp(-v))


def sgn(shape):
    return np.random.uniform(0.5, 2.0, shape) * np.where(np.random.standard_normal(shape) < 0, -1.0, 1.0)


K, T, J, R, N, U, E = 512, 2048, 256, 512, 256, 128, 512


def setup_inputs():
    n = np.random.standard_normal
    idx = np.random.permutation(T)[:J]
    idx2 = np.random.permutation(T)[:J]
    idx3 = np.random.permutation(J)[:U]
    idx4 = np.random.permutation(J)[:U]
    idx5 = np.random.permutation(E)[:U]
    idx6 = np.random.permutation(E)[:J]
    fk = mx_kscale(K)
    fr = mx_kscale(R)
    xtp = pack_weight(n((K, T)) / fk[:, None], "e2m1")
    wp = pack_weight(n((K, R)) * 1 / np.sqrt(K) * fk[:, None] * fr, "e4m3")
    w2p = pack_weight(n((K, R)) * 1 / np.sqrt(K) * fk[:, None] * fr, "e5m2")
    wbp = pack_weight(n((R, N)) * 1 / np.sqrt(R) / fr[:, None], "e2m1")
    wcp = pack_weight(n((R, N)) * 1 / np.sqrt(R) / fr[:, None], "e5m2")
    return {
        "xt_words": xtp[0],
        "xt_scales": xtp[1],
        "w_words": wp[0],
        "w_scales": wp[1],
        "w2_words": w2p[0],
        "w2_scales": w2p[1],
        "wb_words": wbp[0],
        "wb_scales": wbp[1],
        "wc_words": wcp[0],
        "wc_scales": wcp[1],
        "so": (np.random.uniform(0.5, 1.6, (N, 1))).astype(np.float32),
        "sp": (sgn((N, 1))).astype(np.float32),
        "bo": (np.random.uniform(-2.0, 2.0, (N, 1))).astype(np.float32),
        "offs": striped(idx),
        "offs2": striped(idx2),
        "offs3": striped(idx3),
        "offs4": striped(idx4),
        "offs5": striped(idx5),
        "offs6": striped(idx6),
    }


def reference(xt_words, xt_scales, w_words, w_scales, w2_words, w2_scales, wb_words, wb_scales, wc_words, wc_scales, so, sp, bo, offs, offs2, offs3, offs4, offs5, offs6):
    idx = unstriped(offs)
    idx2 = unstriped(offs2)
    idx3 = unstriped(offs3)
    idx4 = unstriped(offs4)
    idx5 = unstriped(offs5)
    idx6 = unstriped(offs6)
    xtu = unpack_weight(xt_words, xt_scales, "e2m1")
    wu = unpack_weight(w_words, w_scales, "e4m3")
    w2u = unpack_weight(w2_words, w2_scales, "e5m2")
    wbu = unpack_weight(wb_words, wb_scales, "e2m1")
    wcu = unpack_weight(wc_words, wc_scales, "e5m2")
    xtidxg = xtu[:, idx]
    a = wu.T @ xtidxg
    xtidx2g = xtu[:, idx2]
    b = w2u.T @ xtidx2g
    hid = np.abs(a - b)
    hidq = mxq(hid, 0, "e5m2")
    p = wbu.T @ hidq
    q = wcu.T @ hidq
    m0 = p[:, idx3] * f64(so) * sigmoid(p[:, idx4] * f64(sp) + f64(bo))
    pw = np.zeros((N, E))
    pw[:, idx5] = m0
    pv = np.zeros((N, E))
    pv[:, idx6] = q
    y = pw + pv
    return y

from contextlib import ExitStack

import concourse.mybir as mybir

K, T, J, R, N, U, E = 512, 2048, 256, 512, 256, 128, 512
FLOPS = 2 * (2 * K * R * J + 2 * R * N * J)

F32 = mybir.dt.float32
BF16 = mybir.dt.bfloat16
I32 = mybir.dt.int32
U32 = mybir.dt.uint32
U16 = mybir.dt.uint16
U8 = mybir.dt.uint8
E4M3X4 = mybir.dt.float8_e4m3fn_x4
E5M2X4 = mybir.dt.float8_e5m2_x4
E2M1X4 = mybir.dt.float4_e2m1fn_x4
ACT = mybir.ActivationFunctionType
ALU = mybir.AluOpType

P = 128
PACK = 4
QUADS = 4
QUAD = 32
HALF = 128
HALVES = J // HALF
PIECE = 64
ROWSETS = N // P


def tile_list_outcomegatedpages_ahead_kernel(
    tc, xt_words, xt_scales, w_words, w_scales, w2_words, w2_scales, wb_words, wb_scales,
    wc_words, wc_scales, so, sp, bo, offs, offs2, offs3, offs4, offs5, offs6, out,
):
    nc = tc.nc
    with ExitStack() as ctx:
        sb = ctx.enter_context(tc.tile_pool(name="sb", bufs=1))
        ps = ctx.enter_context(tc.psum_pool(name="ps", bufs=1))

        def tile(name, shape, dtype, tag=""):
            return sb.tile(shape, dtype, name=name, tag=tag or name, align_bytes=64)

        def load_list(name, src):
            lst = tile(name, list(src.shape), U16)
            nc.sync.dma_start(lst[:], src)
            return lst

        def stage_scales(queue, stage, col, src):
            width = src.shape[2] // 4
            queue.dma_start(
                stage[:, :, col : col + width],
                src[0].bitcast(I32).rearrange("(q r) c -> r q c", r=PACK),
            )

        def spread_scales(plane, stage):
            for q in range(QUADS):
                nc.vector.tensor_copy(plane[QUAD * q : QUAD * q + PACK, :].bitcast(I32), stage[:, q, :])

        xs = tile("xs", [P, T], U8)
        first_plane = tile("first_plane", [P, 2 * R], U8)
        pw = [tile(f"pw{i}", [P, E], F32) for i in range(ROWSETS)]
        pv = [tile(f"pv{i}", [P, E], F32) for i in range(ROWSETS)]
        for plane in (xs, first_plane):
            nc.vector.memset(plane[:].bitcast(I32), 0)
        warm_in = tile("warm_in", [P, 1], F32)
        warm_out = tile("warm_out", [P, 1], F32)
        nc.vector.memset(warm_in[:], 0.0)
        nc.scalar.activation(warm_out[:], warm_in[:], ACT.Sigmoid)
        for page in pv:
            nc.vector.memset(page[:], 0.0)
        for page in pw:
            nc.gpsimd.memset(page[:], 0.0)

        first_stage = tile("first_stage", [PACK, QUADS, 2 * R // 4], I32)
        stage_scales(nc.sync, first_stage, 0, w2_scales)
        stage_scales(nc.sync, first_stage, R // 4, w_scales)
        l2 = load_list("l2", offs2)
        xw = tile("xw", [P, T], U16)
        nc.sync.dma_start(xw[:].bitcast(I32), xt_words[0].bitcast(I32))
        for q in range(QUADS):
            nc.sync.dma_start(
                xs[QUAD * q : QUAD * q + PACK, :].bitcast(I32),
                xt_scales[0, PACK * q : PACK * (q + 1), :].bitcast(I32),
            )
        w2_raw = tile("w2_raw", [P, R], U32)
        w_raw = tile("w_raw", [P, R], U32)
        l1 = load_list("l1", offs)
        nc.sync.dma_start(w2_raw[:].bitcast(I32), w2_words[0].rearrange("p c t -> p (c t)").bitcast(I32))
        nc.sync.dma_start(w_raw[:].bitcast(I32), w_words[0].rearrange("p c t -> p (c t)").bitcast(I32))
        second_stage = tile("second_stage", [PACK, QUADS, 2 * N // 4], I32)
        stage_scales(nc.gpsimd, second_stage, 0, wb_scales)
        stage_scales(nc.gpsimd, second_stage, N // 4, wc_scales)
        wb = tile("wb", [P, 2 * N], U8)
        nc.sync.dma_start(wb[:].bitcast(I32), wb_words[0].bitcast(I32))
        wc = tile("wc", [P, N], U32)
        nc.sync.dma_start(wc[:].bitcast(I32), wc_words[0].rearrange("p c t -> p (c t)").bitcast(I32))
        l6 = load_list("l6", offs6)
        l3 = load_list("l3", offs3)
        l4 = load_list("l4", offs4)
        factors = []
        for name, src in (("so_sb", so), ("sp_sb", sp), ("bo_sb", bo)):
            col = tile(name, [P, ROWSETS], F32)
            with nc.allow_non_contiguous_dma(reason="one float32 a row set and partition"):
                nc.gpsimd.dma_start(col[:], src.rearrange("(i p) o -> p (i o)", p=P))
            factors.append(col)
        so_sb, sp_sb, bo_sb = factors
        l5 = load_list("l5", offs5)

        spread_scales(first_plane, first_stage)
        first_dealt = tile("first_dealt", [P, 2 * R], U8)
        nc.vector.tensor_copy(
            first_dealt[:].rearrange("p (w t m) -> p w t m", w=2, t=PACK),
            first_plane[:].rearrange("p (w m t) -> p w t m", w=2, t=PACK),
        )
        w2_dealt = tile("w2_dealt", [P, R], U32)
        w_dealt = tile("w_dealt", [P, R], U32)
        for dealt, raw in ((w2_dealt, w2_raw), (w_dealt, w_raw)):
            nc.scalar.copy(
                dealt[:].rearrange("p (t m) -> p m t", t=PACK),
                raw[:].rearrange("p (m t) -> p m t", t=PACK),
            )

        picked = []
        for name, lst in (("x2", l2), ("x1", l1)):
            words = tile(name + "_words", [P, J], U16)
            scales = tile(name + "_scales", [P, J], U8)
            nc.vector.tensor_copy(words[:], xw[:].indirect(lst[:]))
            nc.vector.tensor_copy(scales[:], xs[:].indirect(lst[:]))
            picked.append((words, scales))
        (x2_words, x2_scales), (x1_words, x1_scales) = picked

        second_plane = tile("second_plane", [P, 2 * N], U8, tag="xs")
        nc.vector.memset(second_plane[:].bitcast(I32), 0)
        spread_scales(second_plane, second_stage)

        def first_product(name, dealt, fmt, scale_col, words, scales, h):
            bank = ps.tile([P, PACK, HALF], F32, name=name)
            cols = slice(h * HALF, (h + 1) * HALF)
            for t in range(PACK):
                nc.tensor.matmul_mx(
                    out=bank[:, t, :],
                    lhsT=dealt[:, t * P : (t + 1) * P].bitcast(fmt),
                    lhsT_scale=first_dealt[:, scale_col + t * P : scale_col + (t + 1) * P],
                    rhs=words[:, cols].bitcast(E2M1X4),
                    rhs_scale=scales[:, cols],
                    start=True,
                    stop=True,
                )
            return bank

        a_banks, b_sb = [], []
        for h in range(HALVES):
            b_bank = first_product(f"b_bank{h}", w2_dealt, E5M2X4, 0, x2_words, x2_scales, h)
            a_banks.append(first_product(f"a_bank{h}", w_dealt, E4M3X4, R, x1_words, x1_scales, h))
            b_half = tile(f"b_sb{h}", [P, HALF, PACK], F32)
            nc.scalar.copy(b_half[:], b_bank[:].rearrange("p t j -> p j t"))
            b_sb.append(b_half)

        hid = [tile(f"hid{h}", [P, HALF, PACK], BF16) for h in range(HALVES)]
        hid_words = [tile(f"hid_words{h}", [P, HALF], U32) for h in range(HALVES)]
        hid_scales = [tile(f"hid_scales{h}", [P, HALF], U8) for h in range(HALVES)]

        def difference(h, c):
            cols = slice(c * PIECE, (c + 1) * PIECE)
            diff = tile(f"diff{h}_{c}", [P, PIECE, PACK], F32)
            nc.vector.tensor_tensor(
                diff[:], a_banks[h][:].rearrange("p t j -> p j t")[:, cols, :], b_sb[h][:, cols, :], ALU.subtract
            )
            nc.scalar.activation(hid[h][:, cols, :], diff[:], ACT.Abs)

        def quantise(h):
            nc.vector.quantize_mx(
                out=hid_words[h][:].bitcast(E5M2X4),
                scales=hid_scales[h][:],
                in_=hid[h][:].rearrange("p j t -> p (j t)"),
            )

        def second_product(name, operand, scale_col, h):
            bank = ps.tile([P, ROWSETS, HALF], F32, name=name)
            for i in range(ROWSETS):
                nc.tensor.matmul_mx(
                    out=bank[:, i, :],
                    lhsT=operand(i),
                    lhsT_scale=second_plane[:, scale_col + i * P : scale_col + (i + 1) * P],
                    rhs=hid_words[h][:].bitcast(E5M2X4),
                    rhs_scale=hid_scales[h][:],
                    start=True,
                    stop=True,
                )
            return bank

        def p_product(h):
            return second_product(f"p_bank{h}", lambda i: wb[:, 2 * i * P : 2 * (i + 1) * P].bitcast(E2M1X4), 0, h)

        def q_product(h):
            return second_product(f"q_bank{h}", lambda i: wc[:, i * P : (i + 1) * P].bitcast(E5M2X4), N, h)

        p_sb = [tile(f"p_sb{i}", [P, J], F32) for i in range(ROWSETS)]
        q_sb = tile("q_sb", [P, ROWSETS, J], F32)

        def put_q(i, first, last, on_scalar):
            window = pv[i][:].indirect(l6[:, first // 16 : last // 16])
            if on_scalar:
                nc.scalar.activation(window, q_sb[:, i, first:last], ACT.Copy)
            else:
                nc.vector.tensor_copy(window, q_sb[:, i, first:last])

        difference(0, 0)
        difference(0, 1)
        difference(1, 0)
        quantise(0)
        difference(1, 1)
        q_bank0 = q_product(0)
        p_bank0 = p_product(0)
        quantise(1)
        p_bank1 = p_product(1)
        q_bank1 = q_product(1)

        nc.scalar.copy(q_sb[:, :, 0:HALF], q_bank0[:])
        put_q(0, 0, HALF, True)
        for i in range(ROWSETS):
            nc.vector.tensor_copy(p_sb[i][:, 0:HALF], p_bank0[:, i, :])
        put_q(1, 0, PIECE, False)
        for i in range(ROWSETS):
            nc.vector.tensor_copy(p_sb[i][:, HALF:J], p_bank1[:, i, :])
        nc.vector.tensor_copy(q_sb[:, :, HALF:J], q_bank1[:])
        put_q(1, J - PIECE, J, False)

        for i in range(ROWSETS):
            weighted = tile(f"weighted{i}", [P, U], F32)
            gate = tile(f"gate{i}", [P, U], F32)
            nc.scalar.activation(weighted[:], p_sb[i][:].indirect(l3[:]), ACT.Copy, scale=so_sb[:, i : i + 1])
            nc.scalar.activation(
                gate[:], p_sb[i][:].indirect(l4[:]), ACT.Sigmoid, bias=bo_sb[:, i : i + 1], scale=sp_sb[:, i : i + 1]
            )
            nc.vector.tensor_tensor(pw[i][:].indirect(l5[:]), weighted[:], gate[:], ALU.mult)
        put_q(0, HALF, J, True)
        put_q(1, PIECE, J - PIECE, True)

        y0 = tile("y0", [P, E], F32)
        nc.vector.tensor_tensor(y0[:], pw[0][:], pv[0][:], ALU.add)
        nc.sync.dma_start(out[0:P, :], y0[:])
        for c, queue in enumerate((nc.scalar, nc.sync)):
            cols = slice(c * E // 2, (c + 1) * E // 2)
            y1 = tile(f"y1_{c}", [P, E // 2], F32)
            nc.vector.tensor_tensor(y1[:], pw[1][:, cols], pv[1][:, cols], ALU.add)
            queue.dma_start(out[P : 2 * P, cols], y1[:])
